import numpy as np
import ml_dtypes


def mxq(x, axis, fmt="e4m3"):
    dtype, down = {"e4m3": (ml_dtypes.float8_e4m3fn, 7), "e5m2": (ml_dtypes.float8_e5m2, 14)}[fmt]
    v = np.moveaxis(np.asarray(x, np.float32).astype(ml_dtypes.bfloat16).astype(np.float64), axis, -1)
    blocks = v.reshape(v.shape[:-1] + (-1, 32))
    amax = np.abs(blocks).max(-1, keepdims=True)
    byte = np.maximum(np.where(amax > 0, np.frexp(amax)[1] - 1 + 127, 0) - down, 1)
    scale = np.exp2(byte - 127.0)
    codes = (blocks / scale).astype(np.float32).astype(dtype).astype(np.float64)
    return np.moveaxis((codes * scale).reshape(v.shape), -1, axis)


WIDE = False


def mx_kscale(k):
    if not WIDE:
        return np.ones(k)
    levels = np.array([10, -10, 5, -5, 0])
    if k % 512:
        return np.exp2(np.random.permutation(np.resize(levels, k // 32))).repeat(32)
    a = np.empty((k // 512, 16))
    for p in range(k // 512):
        a[p, :8] = np.random.permutation(np.resize(levels, 8))
        for g in range(8):
            far = levels[np.abs(levels - a[p, g]) >= 10]
            a[p, g + 8] = far[np.random.randint(len(far))]
    return np.exp2(a.ravel()).repeat(32)


def f64(x):
    return np.asarray(x).astype(np.float64)


def striped(idx):
    return np.tile(np.asarray(idx).reshape(-1, 16).T, (8, 1)).astype(np.uint16)


def unstriped(offs):
    return offs[:16].T.reshape(-1).astype(np.int64)


E2M1 = np.array([0.0, 0.5, 1.0, 1.5, 2.0, 3.0, 4.0, 6.0, -0.0, -0.5, -1.0, -1.5, -2.0, -3.0, -4.0, -6.0])


def pack_weight(w, fmt):
    k, n = w.shape
    w = f64(np.asarray(w, np.float32).astype(ml_dtypes.bfloat16)).reshape(k // 32, 32, n)
    amax = np.abs(w).max(1)
    if fmt == "e4m3":
        byte = np.frexp(amax)[1] - 1 + 127 - 7
    else:
        mant, ex = np.frexp(amax / 6.0)
        byte = np.where(mant > 0.5, ex, ex - 1) + 127
    byte = np.clip(np.where(amax > 0, byte, 1), 1, 254)
    scaled = (w * np.exp2(127.0 - byte)[:, None, :]).reshape(k, n).astype(np.float32)
    by_word = np.ascontiguousarray(scaled.reshape(k // 512, 128, 4, n).transpose(0, 1, 3, 2))
    if fmt == "e4m3":
        words = by_word.astype(ml_dtypes.float8_e4m3fn).view(np.uint8)
    else:
        c = by_word.astype(ml_dtypes.float4_e2m1fn).view(np.uint8) & 0xF
        words = (c[..., 0::2] | (c[..., 1::2] << 4)).reshape(k // 512, 128, 2 * n)
    return np.ascontiguousarray(words), np.ascontiguousarray(byte.astype(np.uint8).reshape(k // 512, 16, n))


def unpack_weight(words, scales, fmt):
    g, _, n = scales.shape
    words = np.ascontiguousarray(words).reshape(g, 128, n, -1)
    if fmt == "e4m3":
        vals = words.view(ml_dtypes.float8_e4m3fn).astype(np.float64)
    else:
        nib = np.empty((g, 128, n, 4), np.uint8)
        nib[..., 0::2] = words & 0xF
        nib[..., 1::2] = words >> 4
        vals = E2M1[nib]
    vals = vals * np.repeat(np.exp2(scales.astype(np.float64) - 127.0), 8, axis=1)[..., None]
    return vals.transpose(0, 1, 3, 2).reshape(g * 512, n)


D, E, T, I, Q = 512, 512, 2048, 512, 128


def setup_inputs():
    n = np.random.standard_normal
    idx = np.random.permutation(T)[:I]
    fd = mx_kscale(D)
    fe = mx_kscale(E)
    keysp = pack_weight(n((D, T)) / fd[:, None], "e2m1")
    valsp = pack_weight(n((E, T)) / fe[:, None], "e2m1")
    return {
        "query": (n((D, Q)) * 0.4 / np.sqrt(D) * fd[:, None]).astype(np.float32),
        "keys_words": keysp[0],
        "keys_scales": keysp[1],
        "gain": (np.random.uniform(0.3, 0.8, (Q, 1))).astype(np.float32),
        "gout": (n((E, Q)) * 1 / np.sqrt(E) * fe[:, None]).astype(np.float32),
        "vals_words": valsp[0],
        "vals_scales": valsp[1],
        "old": (0.5 * n((Q, T))).astype(np.float32),
        "offs": striped(idx),
    }


def reference(query, keys_words, keys_scales, gain, gout, vals_words, vals_scales, old, offs):
    idx = unstriped(offs)
    keysu = unpack_weight(keys_words, keys_scales, "e2m1")
    valsu = unpack_weight(vals_words, vals_scales, "e2m1")
    queryq = mxq(f64(query), 0, "e4m3")
    keysidxg = keysu[:, idx]
    a = queryq.T @ keysidxg
    p = np.exp(a - np.max(a, axis=1, keepdims=True))
    z = np.sum(p, axis=1, keepdims=True)
    u1 = p / z * f64(gain) * 512.0
    p2 = np.exp(u1 - np.max(u1, axis=1, keepdims=True))
    z2 = np.sum(p2, axis=1, keepdims=True)
    goutq = mxq(f64(gout), 0, "e4m3")
    valsidxg = valsu[:, idx]
    c0 = goutq.T @ valsidxg
    dz2 = np.sum(c0 * p2 / np.square(z2) * (-1.0), axis=1, keepdims=True)
    dp2 = c0 / z2 + dz2
    du1 = dp2 * p2
    dz = np.sum(du1 * 512.0 * f64(gain) * p / np.square(z) * (-1.0), axis=1, keepdims=True)
    dp = du1 * 512.0 * f64(gain) / z + dz
    da = dp * p
    gs = da * 512.0
    gf = np.zeros((Q, T))
    gf[:, idx] = gs
    y = f64(old) + gf
    return y

@@ -1,0 +1,162 @@
+from contextlib import ExitStack
+
+import concourse.mybir as mybir
+
+D, E, T, I, Q = 512, 512, 2048, 512, 128
+FLOPS = 2 * Q * I * (D + E)
+
+F32 = mybir.dt.float32
+BF16 = mybir.dt.bfloat16
+I32 = mybir.dt.int32
+U32 = mybir.dt.uint32
+U16 = mybir.dt.uint16
+U8 = mybir.dt.uint8
+FP8X4 = mybir.dt.float8_e4m3fn_x4
+FP4X4 = mybir.dt.float4_e2m1fn_x4
+ALU = mybir.AluOpType
+EXP = mybir.ActivationFunctionType.Exp
+AXIS_X = mybir.AxisListType.X
+
+P = 128
+PACK = 4
+HALF_I = I // 2
+STORE_WIDTHS = (256, 512, 512, 512, 256)
+
+
+def load_scale_rows(queue, plane, scales):
+    rows = scales[0].bitcast(I32)
+    for quadrant in range(4):
+        queue.dma_start(
+            out=plane[32 * quadrant : 32 * quadrant + 4, :].bitcast(I32),
+            in_=rows[4 * quadrant : 4 * quadrant + 4, :],
+        )
+
+
+def tile_attend_bdoubled_s_kernel(tc, query, keys_words, keys_scales, gain, gout, vals_words, vals_scales, old, offs, out):
+    nc = tc.nc
+    with ExitStack() as ctx:
+        sb = ctx.enter_context(tc.tile_pool(name="sb", bufs=1))
+        psum = ctx.enter_context(tc.psum_pool(name="psum", bufs=1))
+
+        offsets = sb.tile([P, I // 16], U16, name="offsets")
+        nc.sync.dma_start(offsets[:], offs)
+
+        key_scale_pool = sb.tile([P, T], U8, name="key_scale_pool")
+        val_scale_pool = sb.tile([P, T], U8, name="val_scale_pool")
+        spread = sb.tile([P, T], F32, name="spread")
+        nc.vector.memset(key_scale_pool[:].bitcast(I32), 0)
+        nc.vector.memset(val_scale_pool[:].bitcast(I32), 0)
+        nc.vector.memset(spread[:], 0.0)
+
+        key_word_pool = sb.tile([P, T], U16, name="key_word_pool")
+        nc.sync.dma_start(out=key_word_pool[:].bitcast(I32), in_=keys_words[0].bitcast(I32))
+        load_scale_rows(nc.sync, key_scale_pool, keys_scales)
+        query_raw = sb.tile([P, PACK, Q], F32, name="query_raw")
+        nc.sync.dma_start(out=query_raw[:], in_=query.rearrange("(p j) q -> p j q", j=PACK))
+        val_word_pool = sb.tile([P, T], U16, name="val_word_pool")
+        nc.sync.dma_start(out=val_word_pool[:].bitcast(I32), in_=vals_words[0].bitcast(I32))
+        load_scale_rows(nc.sync, val_scale_pool, vals_scales)
+        gout_raw = sb.tile([P, PACK, Q], F32, name="gout_raw", tag="gout_then_p")
+        nc.sync.dma_start(out=gout_raw[:], in_=gout.rearrange("(p j) q -> p j q", j=PACK))
+        gain_col = sb.tile([P, 1], F32, name="gain_col")
+        nc.sync.dma_start(out=gain_col[:], in_=gain)
+        total = sb.tile([P, T], F32, name="total")
+        nc.sync.dma_start(out=total[:], in_=old)
+
+        key_words_g = sb.tile([P, I], U16, name="key_words_g", align_bytes=64)
+        nc.vector.tensor_copy(key_words_g[:], key_word_pool[:].indirect(offsets[:]))
+        key_scales_g = sb.tile([P, I], U8, name="key_scales_g", tag="scales_g", align_bytes=64)
+        nc.vector.tensor_copy(key_scales_g[:], key_scale_pool[:].indirect(offsets[:]))
+
+        query_bf = sb.tile([P, Q, PACK], BF16, name="query_bf", tag="kb", align_bytes=64)
+        nc.scalar.copy(out=query_bf[:], in_=query_raw[:].rearrange("p j q -> p q j"))
+        query_codes = sb.tile([P, Q], U32, name="query_codes", align_bytes=64)
+        query_scales = sb.tile([P, Q], U8, name="query_scales", align_bytes=64)
+        nc.vector.quantize_mx(
+            out=query_codes[:].bitcast(FP8X4), scales=query_scales[:], in_=query_bf[:].rearrange("p q j -> p (q j)")
+        )
+        scores = psum.tile([P, I], F32, name="scores")
+        nc.tensor.matmul_mx(
+            out=scores[:],
+            lhsT=query_codes[:].bitcast(FP8X4),
+            lhsT_scale=query_scales[:],
+            rhs=key_words_g[:].bitcast(FP4X4),
+            rhs_scale=key_scales_g[:],
+            start=True,
+            stop=True,
+        )
+
+        val_words_g = sb.tile([P, I], U16, name="val_words_g", tag="kb", align_bytes=64)
+        nc.vector.tensor_copy(val_words_g[:], val_word_pool[:].indirect(offsets[:]))
+
+        gain512 = sb.tile([P, 1], F32, name="gain512")
+        nc.vector.tensor_scalar(gain512[:], gain_col[:], float(I), None, ALU.mult)
+
+        gout_bf = sb.tile([P, Q, PACK], BF16, name="gout_bf", align_bytes=64)
+        nc.scalar.copy(out=gout_bf[:], in_=gout_raw[:].rearrange("p j q -> p q j"))
+        neg_max = sb.tile([P, 1], F32, name="neg_max")
+        nc.vector.tensor_reduce(neg_max[:], scores[:], AXIS_X, ALU.max, negate=True)
+        p = sb.tile([P, I], F32, name="p", tag="gout_then_p")
+        z = sb.tile([P, 1], F32, name="z")
+        nc.scalar.activation(p[:], scores[:], EXP, bias=neg_max[:], accum_out=z[:])
+
+        val_scales_a = sb.tile([P, HALF_I], U8, name="val_scales_a", tag="scales_g", align_bytes=64)
+        nc.vector.tensor_copy(val_scales_a[:], val_scale_pool[:].indirect(offsets[:, : HALF_I // 16]))
+        gout_codes = sb.tile([P, Q], U32, name="gout_codes", align_bytes=64)
+        gout_scales = sb.tile([P, Q], U8, name="gout_scales", align_bytes=64)
+        nc.vector.quantize_mx(
+            out=gout_codes[:].bitcast(FP8X4), scales=gout_scales[:], in_=gout_bf[:].rearrange("p q j -> p (q j)")
+        )
+
+        rz = sb.tile([P, 1], F32, name="rz")
+        nc.vector.reciprocal(rz[:], z[:])
+        v = sb.tile([P, I], F32, name="v")
+        v_max = sb.tile([P, 1], F32, name="v_max", tag="late", align_bytes=64)
+        nc.vector.tensor_scalar(v[:], p[:], gain512[:], None, ALU.mult, ALU.max, accum_out=v_max[:])
+        neg_u_max = sb.tile([P, 1], F32, name="neg_u_max")
+        nc.vector.tensor_scalar(neg_u_max[:], v_max[:], rz[:], -1.0, ALU.mult, ALU.mult)
+        p2 = sb.tile([P, I], F32, name="p2")
+        z2 = sb.tile([P, 1], F32, name="z2")
+        nc.scalar.activation(p2[:], v[:], EXP, bias=neg_u_max[:], scale=rz[:], accum_out=z2[:])
+
+        val_scales_b = sb.tile([P, HALF_I], U8, name="val_scales_b", tag="late", align_bytes=64)
+        nc.vector.tensor_copy(val_scales_b[:], val_scale_pool[:].indirect(offsets[:, HALF_I // 16 :]))
+        c0 = psum.tile([P, I], F32, name="c0")
+        for half, val_scales_g in enumerate((val_scales_a, val_scales_b)):
+            cols = slice(half * HALF_I, (half + 1) * HALF_I)
+            nc.tensor.matmul_mx(
+                out=c0[:, cols],
+                lhsT=gout_codes[:].bitcast(FP8X4),
+                lhsT_scale=gout_scales[:],
+                rhs=val_words_g[:, cols].bitcast(FP4X4),
+                rhs_scale=val_scales_g[:],
+                start=True,
+                stop=True,
+            )
+        neg_rz = sb.tile([P, 1], F32, name="neg_rz")
+        nc.vector.tensor_scalar(neg_rz[:], rz[:], -1.0, None, ALU.mult)
+
+        rz2 = sb.tile([P, 1], F32, name="rz2")
+        nc.vector.reciprocal(rz2[:], z2[:])
+        factor = sb.tile([P, 1], F32, name="factor")
+        nc.vector.tensor_scalar(factor[:], rz2[:], rz[:], 512.0, ALU.mult, ALU.mult)
+        weight = sb.tile([P, I], F32, name="weight")
+        nc.vector.scalar_tensor_tensor(weight[:], v[:], factor[:], p2[:], ALU.mult, ALU.mult)
+        read_terms = sb.tile([P, I], F32, name="read_terms")
+        c_mean = sb.tile([P, 1], F32, name="c_mean")
+        nc.vector.scalar_tensor_tensor(read_terms[:], c0[:], rz2[:], p2[:], ALU.mult, ALU.mult, accum_out=c_mean[:])
+        direct = sb.tile([P, I], F32, name="direct")
+        direct_sum = sb.tile([P, 1], F32, name="direct_sum")
+        nc.vector.scalar_tensor_tensor(
+            direct[:], c0[:], c_mean[:], weight[:], ALU.subtract, ALU.mult, accum_out=direct_sum[:]
+        )
+        through_z = sb.tile([P, I], F32, name="through_z")
+        nc.vector.tensor_scalar(through_z[:], p[:], direct_sum[:], neg_rz[:], ALU.mult, ALU.mult)
+        nc.vector.tensor_tensor(spread[:].indirect(offsets[:]), direct[:], through_z[:], ALU.add)
+
+        start = 0
+        for width in STORE_WIDTHS:
+            cols = slice(start, start + width)
+            nc.vector.tensor_tensor(total[:, cols], spread[:, cols], total[:, cols], ALU.add)
+            nc.sync.dma_start(out=out[:, cols], in_=total[:, cols])
+            start = start + width

@@ -15,21 +15,19 @@ FP8X4 = mybir.dt.float8_e4m3fn_x4
 FP4X4 = mybir.dt.float4_e2m1fn_x4
 ALU = mybir.AluOpType
 EXP = mybir.ActivationFunctionType.Exp
+COPY = mybir.ActivationFunctionType.Copy
 AXIS_X = mybir.AxisListType.X
 
 P = 128
 PACK = 4
 HALF_I = I // 2
-STORE_WIDTHS = (256, 512, 512, 512, 256)
+STORE_WIDTHS = (192, 256, 320, 384, 448, 448)
 
 
 def load_scale_rows(queue, plane, scales):
     rows = scales[0].bitcast(I32)
-    for quadrant in range(4):
-        queue.dma_start(
-            out=plane[32 * quadrant : 32 * quadrant + 4, :].bitcast(I32),
-            in_=rows[4 * quadrant : 4 * quadrant + 4, :],
-        )
+    for r in range(4):
+        queue.dma_start(out=plane[r:P:32, :].bitcast(I32), in_=rows[r:16:4, :])
 
 
 def tile_attend_bdoubled_s_kernel(tc, query, keys_words, keys_scales, gain, gout, vals_words, vals_scales, old, offs, out):
@@ -51,7 +49,7 @@ def tile_attend_bdoubled_s_kernel(tc, query, keys_words, keys_scales, gain, gout
         key_word_pool = sb.tile([P, T], U16, name="key_word_pool")
         nc.sync.dma_start(out=key_word_pool[:].bitcast(I32), in_=keys_words[0].bitcast(I32))
         load_scale_rows(nc.sync, key_scale_pool, keys_scales)
-        query_raw = sb.tile([P, PACK, Q], F32, name="query_raw")
+        query_raw = sb.tile([P, PACK, Q], F32, name="query_raw", tag="query_then_vw", align_bytes=64)
         nc.sync.dma_start(out=query_raw[:], in_=query.rearrange("(p j) q -> p j q", j=PACK))
         val_word_pool = sb.tile([P, T], U16, name="val_word_pool")
         nc.sync.dma_start(out=val_word_pool[:].bitcast(I32), in_=vals_words[0].bitcast(I32))
@@ -63,12 +61,12 @@ def tile_attend_bdoubled_s_kernel(tc, query, keys_words, keys_scales, gain, gout
         total = sb.tile([P, T], F32, name="total")
         nc.sync.dma_start(out=total[:], in_=old)
 
-        key_words_g = sb.tile([P, I], U16, name="key_words_g", align_bytes=64)
+        key_words_g = sb.tile([P, I], U16, name="key_words_g", tag="kw_then_vs", align_bytes=64)
         nc.vector.tensor_copy(key_words_g[:], key_word_pool[:].indirect(offsets[:]))
-        key_scales_g = sb.tile([P, I], U8, name="key_scales_g", tag="scales_g", align_bytes=64)
+        key_scales_g = sb.tile([P, I], U8, name="key_scales_g", align_bytes=64)
         nc.vector.tensor_copy(key_scales_g[:], key_scale_pool[:].indirect(offsets[:]))
 
-        query_bf = sb.tile([P, Q, PACK], BF16, name="query_bf", tag="kb", align_bytes=64)
+        query_bf = sb.tile([P, Q, PACK], BF16, name="query_bf", align_bytes=64)
         nc.scalar.copy(out=query_bf[:], in_=query_raw[:].rearrange("p j q -> p q j"))
         query_codes = sb.tile([P, Q], U32, name="query_codes", align_bytes=64)
         query_scales = sb.tile([P, Q], U8, name="query_scales", align_bytes=64)
@@ -86,21 +84,21 @@ def tile_attend_bdoubled_s_kernel(tc, query, keys_words, keys_scales, gain, gout
             stop=True,
         )
 
-        val_words_g = sb.tile([P, I], U16, name="val_words_g", tag="kb", align_bytes=64)
+        val_words_g = sb.tile([P, I], U16, name="val_words_g", tag="query_then_vw", align_bytes=64)
         nc.vector.tensor_copy(val_words_g[:], val_word_pool[:].indirect(offsets[:]))
 
         gain512 = sb.tile([P, 1], F32, name="gain512")
-        nc.vector.tensor_scalar(gain512[:], gain_col[:], float(I), None, ALU.mult)
-
+        nc.scalar.mul(gain512[:], gain_col[:], float(I))
         gout_bf = sb.tile([P, Q, PACK], BF16, name="gout_bf", align_bytes=64)
         nc.scalar.copy(out=gout_bf[:], in_=gout_raw[:].rearrange("p j q -> p q j"))
-        neg_max = sb.tile([P, 1], F32, name="neg_max")
+
+        neg_max = sb.tile([P, 1], F32, name="neg_max", tag="max_then_vs", align_bytes=64)
         nc.vector.tensor_reduce(neg_max[:], scores[:], AXIS_X, ALU.max, negate=True)
         p = sb.tile([P, I], F32, name="p", tag="gout_then_p")
         z = sb.tile([P, 1], F32, name="z")
         nc.scalar.activation(p[:], scores[:], EXP, bias=neg_max[:], accum_out=z[:])
 
-        val_scales_a = sb.tile([P, HALF_I], U8, name="val_scales_a", tag="scales_g", align_bytes=64)
+        val_scales_a = sb.tile([P, HALF_I], U8, name="val_scales_a", tag="kw_then_vs", align_bytes=64)
         nc.vector.tensor_copy(val_scales_a[:], val_scale_pool[:].indirect(offsets[:, : HALF_I // 16]))
         gout_codes = sb.tile([P, Q], U32, name="gout_codes", align_bytes=64)
         gout_scales = sb.tile([P, Q], U8, name="gout_scales", align_bytes=64)
@@ -111,15 +109,17 @@ def tile_attend_bdoubled_s_kernel(tc, query, keys_words, keys_scales, gain, gout
         rz = sb.tile([P, 1], F32, name="rz")
         nc.vector.reciprocal(rz[:], z[:])
         v = sb.tile([P, I], F32, name="v")
-        v_max = sb.tile([P, 1], F32, name="v_max", tag="late", align_bytes=64)
+        v_max = sb.tile([P, 1], F32, name="v_max")
         nc.vector.tensor_scalar(v[:], p[:], gain512[:], None, ALU.mult, ALU.max, accum_out=v_max[:])
+        neg_rz = sb.tile([P, 1], F32, name="neg_rz")
+        nc.scalar.mul(neg_rz[:], rz[:], -1.0)
         neg_u_max = sb.tile([P, 1], F32, name="neg_u_max")
-        nc.vector.tensor_scalar(neg_u_max[:], v_max[:], rz[:], -1.0, ALU.mult, ALU.mult)
+        nc.scalar.activation(neg_u_max[:], v_max[:], COPY, scale=neg_rz[:])
         p2 = sb.tile([P, I], F32, name="p2")
         z2 = sb.tile([P, 1], F32, name="z2")
         nc.scalar.activation(p2[:], v[:], EXP, bias=neg_u_max[:], scale=rz[:], accum_out=z2[:])
 
-        val_scales_b = sb.tile([P, HALF_I], U8, name="val_scales_b", tag="late", align_bytes=64)
+        val_scales_b = sb.tile([P, HALF_I], U8, name="val_scales_b", tag="max_then_vs", align_bytes=64)
         nc.vector.tensor_copy(val_scales_b[:], val_scale_pool[:].indirect(offsets[:, HALF_I // 16 :]))
         c0 = psum.tile([P, I], F32, name="c0")
         for half, val_scales_g in enumerate((val_scales_a, val_scales_b)):
@@ -133,18 +133,16 @@ def tile_attend_bdoubled_s_kernel(tc, query, keys_words, keys_scales, gain, gout
                 start=True,
                 stop=True,
             )
-        neg_rz = sb.tile([P, 1], F32, name="neg_rz")
-        nc.vector.tensor_scalar(neg_rz[:], rz[:], -1.0, None, ALU.mult)
 
         rz2 = sb.tile([P, 1], F32, name="rz2")
         nc.vector.reciprocal(rz2[:], z2[:])
         factor = sb.tile([P, 1], F32, name="factor")
         nc.vector.tensor_scalar(factor[:], rz2[:], rz[:], 512.0, ALU.mult, ALU.mult)
-        weight = sb.tile([P, I], F32, name="weight")
-        nc.vector.scalar_tensor_tensor(weight[:], v[:], factor[:], p2[:], ALU.mult, ALU.mult)
         read_terms = sb.tile([P, I], F32, name="read_terms")
         c_mean = sb.tile([P, 1], F32, name="c_mean")
         nc.vector.scalar_tensor_tensor(read_terms[:], c0[:], rz2[:], p2[:], ALU.mult, ALU.mult, accum_out=c_mean[:])
+        weight = sb.tile([P, I], F32, name="weight")
+        nc.vector.scalar_tensor_tensor(weight[:], v[:], factor[:], p2[:], ALU.mult, ALU.mult)
         direct = sb.tile([P, I], F32, name="direct")
         direct_sum = sb.tile([P, 1], F32, name="direct_sum")
         nc.vector.scalar_tensor_tensor(

@@ -42,8 +42,8 @@ def tile_attend_bdoubled_s_kernel(tc, query, keys_words, keys_scales, gain, gout
         key_scale_pool = sb.tile([P, T], U8, name="key_scale_pool")
         val_scale_pool = sb.tile([P, T], U8, name="val_scale_pool")
         spread = sb.tile([P, T], F32, name="spread")
-        nc.vector.memset(key_scale_pool[:].bitcast(I32), 0)
-        nc.vector.memset(val_scale_pool[:].bitcast(I32), 0)
+        nc.gpsimd.memset(key_scale_pool[:].bitcast(I32), 0)
+        nc.gpsimd.memset(val_scale_pool[:].bitcast(I32), 0)
         nc.vector.memset(spread[:], 0.0)
 
         key_word_pool = sb.tile([P, T], U16, name="key_word_pool")
@@ -153,8 +153,8 @@ def tile_attend_bdoubled_s_kernel(tc, query, keys_words, keys_scales, gain, gout
         nc.vector.tensor_tensor(spread[:].indirect(offsets[:]), direct[:], through_z[:], ALU.add)
 
         start = 0
-        for width in STORE_WIDTHS:
+        for piece, width in enumerate(STORE_WIDTHS):
             cols = slice(start, start + width)
             nc.vector.tensor_tensor(total[:, cols], spread[:, cols], total[:, cols], ALU.add)
-            nc.sync.dma_start(out=out[:, cols], in_=total[:, cols])
+            (nc.sync, nc.scalar)[piece % 2].dma_start(out=out[:, cols], in_=total[:, cols])
             start = start + width

from contextlib import ExitStack

import concourse.mybir as mybir

D, E, T, I, Q = 512, 512, 2048, 512, 128
FLOPS = 2 * Q * I * (D + E)

F32 = mybir.dt.float32
BF16 = mybir.dt.bfloat16
I32 = mybir.dt.int32
U32 = mybir.dt.uint32
U16 = mybir.dt.uint16
U8 = mybir.dt.uint8
FP8X4 = mybir.dt.float8_e4m3fn_x4
FP4X4 = mybir.dt.float4_e2m1fn_x4
ALU = mybir.AluOpType
EXP = mybir.ActivationFunctionType.Exp
COPY = mybir.ActivationFunctionType.Copy
AXIS_X = mybir.AxisListType.X

P = 128
PACK = 4
HALF_I = I // 2
STORE_WIDTHS = (192, 256, 320, 384, 448, 448)


def load_scale_rows(queue, plane, scales):
    rows = scales[0].bitcast(I32)
    for r in range(4):
        queue.dma_start(out=plane[r:P:32, :].bitcast(I32), in_=rows[r:16:4, :])


def tile_attend_bdoubled_s_kernel(tc, query, keys_words, keys_scales, gain, gout, vals_words, vals_scales, old, offs, out):
    nc = tc.nc
    with ExitStack() as ctx:
        sb = ctx.enter_context(tc.tile_pool(name="sb", bufs=1))
        psum = ctx.enter_context(tc.psum_pool(name="psum", bufs=1))

        offsets = sb.tile([P, I // 16], U16, name="offsets")
        nc.sync.dma_start(offsets[:], offs)

        key_scale_pool = sb.tile([P, T], U8, name="key_scale_pool")
        val_scale_pool = sb.tile([P, T], U8, name="val_scale_pool")
        spread = sb.tile([P, T], F32, name="spread")
        nc.gpsimd.memset(key_scale_pool[:].bitcast(I32), 0)
        nc.gpsimd.memset(val_scale_pool[:].bitcast(I32), 0)
        nc.vector.memset(spread[:], 0.0)

        key_word_pool = sb.tile([P, T], U16, name="key_word_pool")
        nc.sync.dma_start(out=key_word_pool[:].bitcast(I32), in_=keys_words[0].bitcast(I32))
        load_scale_rows(nc.sync, key_scale_pool, keys_scales)
        query_raw = sb.tile([P, PACK, Q], F32, name="query_raw", tag="query_then_vw", align_bytes=64)
        nc.sync.dma_start(out=query_raw[:], in_=query.rearrange("(p j) q -> p j q", j=PACK))
        val_word_pool = sb.tile([P, T], U16, name="val_word_pool")
        nc.sync.dma_start(out=val_word_pool[:].bitcast(I32), in_=vals_words[0].bitcast(I32))
        load_scale_rows(nc.sync, val_scale_pool, vals_scales)
        gout_raw = sb.tile([P, PACK, Q], F32, name="gout_raw", tag="gout_then_p")
        nc.sync.dma_start(out=gout_raw[:], in_=gout.rearrange("(p j) q -> p j q", j=PACK))
        gain_col = sb.tile([P, 1], F32, name="gain_col")
        nc.sync.dma_start(out=gain_col[:], in_=gain)
        total = sb.tile([P, T], F32, name="total")
        nc.sync.dma_start(out=total[:], in_=old)

        key_words_g = sb.tile([P, I], U16, name="key_words_g", tag="kw_then_vs", align_bytes=64)
        nc.vector.tensor_copy(key_words_g[:], key_word_pool[:].indirect(offsets[:]))
        key_scales_g = sb.tile([P, I], U8, name="key_scales_g", align_bytes=64)
        nc.vector.tensor_copy(key_scales_g[:], key_scale_pool[:].indirect(offsets[:]))

        query_bf = sb.tile([P, Q, PACK], BF16, name="query_bf", align_bytes=64)
        nc.scalar.copy(out=query_bf[:], in_=query_raw[:].rearrange("p j q -> p q j"))
        query_codes = sb.tile([P, Q], U32, name="query_codes", align_bytes=64)
        query_scales = sb.tile([P, Q], U8, name="query_scales", align_bytes=64)
        nc.vector.quantize_mx(
            out=query_codes[:].bitcast(FP8X4), scales=query_scales[:], in_=query_bf[:].rearrange("p q j -> p (q j)")
        )
        scores = psum.tile([P, I], F32, name="scores")
        nc.tensor.matmul_mx(
            out=scores[:],
            lhsT=query_codes[:].bitcast(FP8X4),
            lhsT_scale=query_scales[:],
            rhs=key_words_g[:].bitcast(FP4X4),
            rhs_scale=key_scales_g[:],
            start=True,
            stop=True,
        )

        val_words_g = sb.tile([P, I], U16, name="val_words_g", tag="query_then_vw", align_bytes=64)
        nc.vector.tensor_copy(val_words_g[:], val_word_pool[:].indirect(offsets[:]))

        gain512 = sb.tile([P, 1], F32, name="gain512")
        nc.scalar.mul(gain512[:], gain_col[:], float(I))
        gout_bf = sb.tile([P, Q, PACK], BF16, name="gout_bf", align_bytes=64)
        nc.scalar.copy(out=gout_bf[:], in_=gout_raw[:].rearrange("p j q -> p q j"))

        neg_max = sb.tile([P, 1], F32, name="neg_max", tag="max_then_vs", align_bytes=64)
        nc.vector.tensor_reduce(neg_max[:], scores[:], AXIS_X, ALU.max, negate=True)
        p = sb.tile([P, I], F32, name="p", tag="gout_then_p")
        z = sb.tile([P, 1], F32, name="z")
        nc.scalar.activation(p[:], scores[:], EXP, bias=neg_max[:], accum_out=z[:])

        val_scales_a = sb.tile([P, HALF_I], U8, name="val_scales_a", tag="kw_then_vs", align_bytes=64)
        nc.vector.tensor_copy(val_scales_a[:], val_scale_pool[:].indirect(offsets[:, : HALF_I // 16]))
        gout_codes = sb.tile([P, Q], U32, name="gout_codes", align_bytes=64)
        gout_scales = sb.tile([P, Q], U8, name="gout_scales", align_bytes=64)
        nc.vector.quantize_mx(
            out=gout_codes[:].bitcast(FP8X4), scales=gout_scales[:], in_=gout_bf[:].rearrange("p q j -> p (q j)")
        )

        rz = sb.tile([P, 1], F32, name="rz")
        nc.vector.reciprocal(rz[:], z[:])
        v = sb.tile([P, I], F32, name="v")
        v_max = sb.tile([P, 1], F32, name="v_max")
        nc.vector.tensor_scalar(v[:], p[:], gain512[:], None, ALU.mult, ALU.max, accum_out=v_max[:])
        neg_rz = sb.tile([P, 1], F32, name="neg_rz")
        nc.scalar.mul(neg_rz[:], rz[:], -1.0)
        neg_u_max = sb.tile([P, 1], F32, name="neg_u_max")
        nc.scalar.activation(neg_u_max[:], v_max[:], COPY, scale=neg_rz[:])
        p2 = sb.tile([P, I], F32, name="p2")
        z2 = sb.tile([P, 1], F32, name="z2")
        nc.scalar.activation(p2[:], v[:], EXP, bias=neg_u_max[:], scale=rz[:], accum_out=z2[:])

        val_scales_b = sb.tile([P, HALF_I], U8, name="val_scales_b", tag="max_then_vs", align_bytes=64)
        nc.vector.tensor_copy(val_scales_b[:], val_scale_pool[:].indirect(offsets[:, HALF_I // 16 :]))
        c0 = psum.tile([P, I], F32, name="c0")
        for half, val_scales_g in enumerate((val_scales_a, val_scales_b)):
            cols = slice(half * HALF_I, (half + 1) * HALF_I)
            nc.tensor.matmul_mx(
                out=c0[:, cols],
                lhsT=gout_codes[:].bitcast(FP8X4),
                lhsT_scale=gout_scales[:],
                rhs=val_words_g[:, cols].bitcast(FP4X4),
                rhs_scale=val_scales_g[:],
                start=True,
                stop=True,
            )

        rz2 = sb.tile([P, 1], F32, name="rz2")
        nc.vector.reciprocal(rz2[:], z2[:])
        factor = sb.tile([P, 1], F32, name="factor")
        nc.vector.tensor_scalar(factor[:], rz2[:], rz[:], 512.0, ALU.mult, ALU.mult)
        read_terms = sb.tile([P, I], F32, name="read_terms")
        c_mean = sb.tile([P, 1], F32, name="c_mean")
        nc.vector.scalar_tensor_tensor(read_terms[:], c0[:], rz2[:], p2[:], ALU.mult, ALU.mult, accum_out=c_mean[:])
        weight = sb.tile([P, I], F32, name="weight")
        nc.vector.scalar_tensor_tensor(weight[:], v[:], factor[:], p2[:], ALU.mult, ALU.mult)
        direct = sb.tile([P, I], F32, name="direct")
        direct_sum = sb.tile([P, 1], F32, name="direct_sum")
        nc.vector.scalar_tensor_tensor(
            direct[:], c0[:], c_mean[:], weight[:], ALU.subtract, ALU.mult, accum_out=direct_sum[:]
        )
        through_z = sb.tile([P, I], F32, name="through_z")
        nc.vector.tensor_scalar(through_z[:], p[:], direct_sum[:], neg_rz[:], ALU.mult, ALU.mult)
        nc.vector.tensor_tensor(spread[:].indirect(offsets[:]), direct[:], through_z[:], ALU.add)

        start = 0
        for piece, width in enumerate(STORE_WIDTHS):
            cols = slice(start, start + width)
            nc.vector.tensor_tensor(total[:, cols], spread[:, cols], total[:, cols], ALU.add)
            (nc.sync, nc.scalar)[piece % 2].dma_start(out=out[:, cols], in_=total[:, cols])
            start = start + width
